import numpy as np, ml_dtypes
CORES = [56,64,184,192,312,320,440,448]
N = 8
import mx_ref
NC, G = 256, 2
C = np.float32(0.041)
BF = ml_dtypes.bfloat16
def cut(t, i, w=512):
    return t[:, w * i:w * i + w]
def tile(rs):
    return np.stack(rs, axis=2).reshape(128, -1).astype(BF)
def act(Z):
    return [np.maximum(s * z, 0) * C for z in Z for s in (1, -1)]
def setup_inputs(rng):
    def f(*shape):
        return mx_ref.flush((rng.standard_normal(shape, dtype=np.float32) * np.exp2(rng.integers(-2, 3, shape[:-1] + (1,)))).astype(BF))
    return {"x": f(N, 128, 4 * NC), "res": f(N, 128, 4 * NC), "w1": f(N, 128, 512), "w2": f(N, 128, 2 * 512)}
def setup_inputs_blocks(rng):
    d = setup_inputs(rng)
    for k in ("x", "w1", "w2", "res"): d[k] = mx_ref.spread(d[k], rng, 4)
    return d
def setup_inputs_wide(rng):
    d = setup_inputs(rng)
    for k in ("x", "w1", "w2", "res"): d[k] = mx_ref.flush((d[k].astype(np.float32) * np.exp2(rng.integers(-6, 7, (N, 1, 1))).astype(np.float32)).astype(BF))
    return d
def reference(x, res, w1, w2):
    W = [mx_ref.quantize(w1[j]) for j in range(N)]; H = []
    for r in range(N):
        X = mx_ref.quantize(x[r]); e = res[r].astype(np.float32)
        R = act([mx_ref.matmul(W[(r + i) % N], X) for i in range(G)])
        H.append(mx_ref.quantize(tile([R[b] + e[:, b::4] for b in range(4)])))
    y = np.zeros((N, 128, NC), np.float32)
    for r in range(N):
        y[r] = mx_ref.matmul(mx_ref.quantize(cut(w2[r], 0)), H[r]) + mx_ref.matmul(mx_ref.quantize(cut(w2[r], 1)), H[(r + 1) % N])
    return {"y": y}

import numpy as np
from concourse.bass import DstId, RemoteDMATransfer
from concourse.mybir import dt, AluOpType, ActivationFunctionType

N = 8
WORLD = 512
NC = 256
BANK = 512
CHUNKS = ((0, 128), (128, 256))
C = float(np.float32(0.041))

SCRATCH = {
    "w1t": ("sbuf", [128, 512], "bfloat16"),
    "xt": ("sbuf", [128, 4 * NC], "bfloat16"),
    "rt": ("sbuf", [128, 4 * NC], "bfloat16"),
    "w2t": ("sbuf", [128, 1024], "bfloat16"),
    "ht": ("sbuf", [128, 4 * NC], "bfloat16"),
    "w1q": ("sbuf", [128, 128], "float8_e4m3fn_x4"), "w1s": ("sbuf", [128, 128], "uint8"),
    "xq": ("sbuf", [128, NC], "float8_e4m3fn_x4"), "xs": ("sbuf", [128, NC], "uint8"),
    "w2q": ("sbuf", [128, 256], "float8_e4m3fn_x4"), "w2s": ("sbuf", [128, 256], "uint8"),
    "hq": ("sbuf", [128, NC], "float8_e4m3fn_x4"), "hs": ("sbuf", [128, NC], "uint8"),
    "w1nq": ("sbuf", [128, 128], "float8_e4m3fn_x4"), "w1ns": ("sbuf", [128, 128], "uint8"),
    "hnq": ("sbuf", [128, NC], "float8_e4m3fn_x4"), "hns": ("sbuf", [128, NC], "uint8"),
    "tmp": ("sbuf", [128, 4 * NC], "float32"),
    "yt": ("sbuf", [128, NC], "float32"),
    "z0": ("psum", [128, BANK], "float32"),
    "z1": ("psum", [128, BANK * len(CHUNKS)], "float32"),
    "yp": ("psum", [128, BANK * len(CHUNKS)], "float32"),
}

SEMAPHORES = (["ld_w1", "ld_x", "ld_res", "ld_w2", "q_w1", "q_x", "q_w2", "m_z0", "r0", "r1", "a_pre", "ar_w1", "ls", "st_y"]
              + [n + str(i) for i in range(len(CHUNKS)) for n in ("m_z1", "r2", "r3", "a", "q_h", "ar_h", "m_y", "c_y")])

ROUTE = {
    "w1": [[("w1", "q", 0, 128, 0, (0, 2))],
           [("w1", "s", 0, 64, 1, (2, 4)), ("w1", "s", 64, 128, 2, (3, 4))]],
    "h0": [[("h", "q", 0, 128, 0, (0, 1))], [("h", "s", 0, 128, 1, (0, 1))]],
    "h1": [[("h", "q", 128, 256, 2, (0, 1))], [("h", "s", 128, 256, 1, (0, 1))]],
}
GROUPS = ("w1", "h0", "h1")
ARRIVE = {"w1": "ar_w1", "h0": "ar_h0", "h1": "ar_h1"}

_CACHE = {}


def _engines(mask):
    return [e for e in range(mask.bit_length()) if (mask >> e) & 1]


def _share(mask, part):
    k, parts = part
    engs = _engines(mask)
    n = len(engs) // parts
    m = 0
    for e in engs[k * n:(k + 1) * n]:
        m |= 1 << e
    return m, n


def _view(T, name, kind, c0, c1):
    v = T[name + kind][:, c0:c1]
    return v.bitcast(dt.uint8) if kind == "q" else v


def _plan(T, topo):
    if "plan" not in _CACHE:
        ranks, relays = {}, {}
        for s in range(N):
            src, dst = T.cores[s], T.cores[(s - 1) % N]
            cand = [d for d in range(WORLD)
                    if d != src and topo.host(d) == topo.host(src) and topo.chip(d) == topo.chip(src)
                    and T.rank_of(d) is None and topo.may_write(src, d) and topo.may_write(d, dst)]
            slots = ([d for d in cand if topo.die(d) == topo.die(src)] + [d for d in cand if topo.die(d) != topo.die(src)])
            ranks[src] = slots
            for k, d in enumerate(slots):
                relays[d] = (src, dst, k)
        _CACHE["plan"] = (ranks, relays)
    return _CACHE["plan"]


def _forward(g, core, T, topo, src, dst, slot):
    rid, pid = topo.addr(dst, core)
    out_mask, out_n = _share(topo.mask(core, dst), (0, 1))
    sent = 0
    for grp in GROUPS:
        for call in ROUTE[grp]:
            for (name, kind, c0, c1, sl, part) in call:
                if sl != slot:
                    continue
                g.wait_ge(T.sem[ARRIVE[grp]], _share(topo.mask(src, core), part)[1])
                g.remote_dma(_view(T, name + "n", kind, c0, c1), _view(T, name + "n", kind, c0, c1),
                             T.sem[ARRIVE[grp]], T.sem.ls, pid, rid, out_mask)
                sent += out_n
    if sent:
        g.wait_ge(T.sem.ls, sent)


def _send(g, core, T, topo, slots, grp):
    left = 0
    for call in ROUTE[grp]:
        trs = []
        for (name, kind, c0, c1, sl, part) in call:
            rid, pid = topo.addr(slots[sl], core)
            m, n = _share(topo.mask(core, slots[sl]), part)
            trs.append((_view(T, name + "n", kind, c0, c1), _view(T, name, kind, c0, c1), pid, rid, m))
            left += n
        if len(trs) == 1:
            o, i, pid, rid, m = trs[0]
            g.remote_dma(o, i, T.sem[ARRIVE[grp]], T.sem.ls, pid, rid, m)
        else:
            g.remote_dma_fused([RemoteDMATransfer(dst_ids=[DstId(rid=rid, pnc=pid)], dma_engine_mask=m,
                                                  remote_sem=T.sem[ARRIVE[grp]], src=i, dst=o)
                                for (o, i, pid, rid, m) in trs], local_sem=T.sem.ls)
    return left


def _arrivals(T, topo, core, grp):
    ranks, relays = _plan(T, topo)
    up = T.cores[(T.rank_of(core) + 1) % N]
    return sum(_share(topo.mask(ranks[up][p[4]], core), (0, 1))[1] for call in ROUTE[grp] for p in call)


def _rank(g, core, T, topo, slots):
    S = T.sem
    v, a, t, sy = g.vector, g.scalar, g.tensor, g.sync
    relu, add = ActivationFunctionType.Relu, AluOpType.add
    nch = len(CHUNKS)

    sy.dma_start(T.w1t[:], T.w1[:]).then_inc(S.ld_w1, 16)
    sy.dma_start(T.xt[:], T.x[:]).then_inc(S.ld_x, 16)
    sy.dma_start(T.rt[:], T.res[:]).then_inc(S.ld_res, 16)
    sy.dma_start(T.w2t[:], T.w2[:]).then_inc(S.ld_w2, 16)

    g.wait_ge(S.q_w1, 1)
    left = _send(g, core, T, topo, slots, "w1")
    for i in range(nch):
        g.wait_ge(S["q_h%d" % i], 1)
        left += _send(g, core, T, topo, slots, "h%d" % i)
    g.wait_ge(S.ls, left)

    v.wait_ge(S.ld_w1, 16)
    v.quantize_mx(T.w1q[:], T.w1s[:], T.w1t[:]).then_inc(S.q_w1, 1)
    v.wait_ge(S.ld_x, 16)
    v.quantize_mx(T.xq[:], T.xs[:], T.xt[:]).then_inc(S.q_x, 1)
    v.wait_ge(S.ld_w2, 16)
    v.quantize_mx(T.w2q[:], T.w2s[:], T.w2t[:]).then_inc(S.q_w2, 1)
    v.wait_ge(S.ld_res, 16)
    for b in (0, 1):
        v.wait_ge(S["r%d" % b], 1)
        v.tensor_tensor(T.ht[:, b:4 * NC:4], T.tmp[:, NC * b:NC * (b + 1)], T.rt[:, b:4 * NC:4], add).then_inc(S.a_pre, 1)
    v.wait_ge(S.a_pre, 2)
    for i, (c0, c1) in enumerate(CHUNKS):
        for b in (2, 3):
            v.wait_ge(S["r%d%d" % (b, i)], 1)
            v.tensor_tensor(T.ht[:, 4 * c0 + b:4 * c1:4], T.tmp[:, NC * b + c0:NC * b + c1], T.rt[:, 4 * c0 + b:4 * c1:4],
                            add).then_inc(S["a%d" % i], 1)
        v.wait_ge(S["a%d" % i], 2)
        v.quantize_mx(T.hq[:, c0:c1], T.hs[:, c0:c1], T.ht[:, 4 * c0:4 * c1]).then_inc(S["q_h%d" % i], 1)
    for i, (c0, c1) in enumerate(CHUNKS):
        v.wait_ge(S["m_y%d" % i], 1)
        v.tensor_copy(T.yt[:, c0:c1], T.yp[:, BANK * i:BANK * i + c1 - c0]).then_inc(S["c_y%d" % i], 1)

    a.wait_ge(S.m_z0, 1)
    a.activation(T.tmp[:, 0:NC], T.z0[:, 0:NC], relu, scale=C).then_inc(S.r0, 1)
    a.activation(T.tmp[:, NC:2 * NC], T.z0[:, 0:NC], relu, scale=-C).then_inc(S.r1, 1)
    for i, (c0, c1) in enumerate(CHUNKS):
        a.wait_ge(S["m_z1%d" % i], 1)
        z = T.z1[:, BANK * i:BANK * i + c1 - c0]
        a.activation(T.tmp[:, 2 * NC + c0:2 * NC + c1], z, relu, scale=C).then_inc(S["r2%d" % i], 1)
        a.activation(T.tmp[:, 3 * NC + c0:3 * NC + c1], z, relu, scale=-C).then_inc(S["r3%d" % i], 1)

    t.wait_ge(S.q_w1, 1)
    t.wait_ge(S.q_x, 1)
    t.matmul_mx(T.z0[:, 0:NC], T.w1q[:], T.w1s[:], T.xq[:], T.xs[:], True, True).then_inc(S.m_z0, 1)
    t.wait_ge(S.ar_w1, _arrivals(T, topo, core, "w1"))
    for i, (c0, c1) in enumerate(CHUNKS):
        t.matmul_mx(T.z1[:, BANK * i:BANK * i + c1 - c0], T.w1nq[:], T.w1ns[:], T.xq[:, c0:c1], T.xs[:, c0:c1],
                    True, True).then_inc(S["m_z1%d" % i], 1)
    t.wait_ge(S.q_w2, 1)
    for i, (c0, c1) in enumerate(CHUNKS):
        t.wait_ge(S["q_h%d" % i], 1)
        t.matmul_mx(T.yp[:, BANK * i:BANK * i + c1 - c0], T.w2q[:, 0:128], T.w2s[:, 0:128], T.hq[:, c0:c1], T.hs[:, c0:c1],
                    True, False)
    for i, (c0, c1) in enumerate(CHUNKS):
        t.wait_ge(S["ar_h%d" % i], _arrivals(T, topo, core, "h%d" % i))
        t.matmul_mx(T.yp[:, BANK * i:BANK * i + c1 - c0], T.w2q[:, 128:256], T.w2s[:, 128:256], T.hnq[:, c0:c1],
                    T.hns[:, c0:c1], False, True).then_inc(S["m_y%d" % i], 1)

    for i, (c0, c1) in enumerate(CHUNKS):
        sy.wait_ge(S["c_y%d" % i], 1)
        sy.dma_start(T.y[:, c0:c1], T.yt[:, c0:c1]).then_inc(S.st_y, 16)
    sy.wait_ge(S.st_y, 16 * nch)


def rank_program(g, core, T, topo):
    ranks, relays = _plan(T, topo)
    if core in ranks:
        _rank(g, core, T, topo, ranks[core])
    elif core in relays:
        _forward(g, core, T, topo, *relays[core])
